import numpy as np
import ml_dtypes

BF16 = ml_dtypes.bfloat16


def bf(x):
    return np.asarray(x, np.float32).astype(BF16)


def f32(x):
    return np.asarray(x, np.float32)


def f64(x):
    return np.asarray(x).astype(np.float64)


def striped(idx):
    return np.tile(idx.reshape(-1, 16).T, (8, 1))


S, K, M, N, D, V = 512, 256, 256, 768, 8, 96


def gelu_tanh(v):
    return 0.5 * v * (1.0 + np.tanh(np.sqrt(2.0 / np.pi) * (v + 0.044715 * v**3)))


def setup_inputs():
    return {"table": bf(np.random.standard_normal((S, K))), "w": bf(np.random.standard_normal((K, M)) / np.sqrt(K)), "b": f32(0.5 * np.random.standard_normal((M, 1))), "offs": striped(np.random.permutation(np.tile(np.arange(S), 2))[:N])}


def reference(table, w, b, offs):
    idx = offs[:16].T.reshape(-1)
    x = f64(table)[idx].T
    y = f64(w).T @ x
    z = gelu_tanh(y + f64(b))
    return z.reshape(M, V, D).max(axis=2)

@@ -1,0 +1,78 @@
+import concourse.mybir as mybir
+from concourse.masks import make_identity
+
+F32, BF16, U16 = mybir.dt.float32, mybir.dt.bfloat16, mybir.dt.uint16
+GELU = mybir.ActivationFunctionType.Gelu_apprx_tanh
+
+P = 128
+NODES, FEATURES, OUTPUTS = 512, 256, 256
+ENTRIES, NEIGHBOURS = 768, 8
+PIECE = 256
+NODE_BLOCKS, K_BLOCKS, M_BLOCKS = NODES // P, FEATURES // P, OUTPUTS // P
+PIECES = ENTRIES // PIECE
+PIECE_OFFS = PIECE // 16
+PIECE_POOLED = PIECE // NEIGHBOURS
+POOLED = ENTRIES // NEIGHBOURS
+
+FLOPS = 2 * FEATURES * OUTPUTS * ENTRIES
+
+
+def tile_gather_matmul_kernel(tc, table, w, b, offs, out):
+    nc = tc.nc
+    with (
+        tc.tile_pool(name="held", bufs=1) as held,
+        tc.tile_pool(name="epilogue", bufs=PIECES * M_BLOCKS) as epilogue,
+        tc.psum_pool(name="flip_psum", bufs=1) as flip_psum,
+        tc.psum_pool(name="sum_psum", bufs=PIECES * M_BLOCKS) as sum_psum,
+    ):
+        rows = held.tile([P, NODE_BLOCKS, FEATURES], BF16)
+        nc.sync.dma_start(rows[:], table.rearrange("(n p) k -> p n k", p=P))
+        offsets = held.tile([P, ENTRIES // 16], U16)
+        nc.sync.dma_start(offsets[:], offs)
+        weights = held.tile([P, K_BLOCKS, OUTPUTS], BF16)
+        nc.scalar.dma_start(weights[:], w.rearrange("(k p) m -> p k m", p=P))
+        bias = held.tile([P, M_BLOCKS], F32)
+        nc.scalar.dma_start(bias[:], b.rearrange("(m p) o -> p (m o)", p=P))
+
+        identity = held.tile([P, P], BF16)
+        make_identity(nc, identity[:])
+
+        zero = held.tile([P, 1], F32)
+        nc.vector.memset(zero[:], 0.0)
+        warm = held.tile([P, 1], F32)
+        nc.scalar.activation(warm[:], zero[:], GELU, bias=zero[:])
+
+        windows = []
+        for k in range(K_BLOCKS):
+            flipped = flip_psum.tile([P, NODES], BF16, name=f"flipped{k}")
+            for n in range(NODE_BLOCKS):
+                nc.tensor.transpose(flipped[:, n * P : (n + 1) * P], rows[:, n, k * P : (k + 1) * P], identity[:])
+            window = held.tile([P, NODES], BF16, name=f"window{k}")
+            if k % 2 == 0:
+                nc.vector.tensor_copy(window[:], flipped[:])
+            else:
+                nc.scalar.copy(window[:], flipped[:])
+            windows.append(window)
+
+        for m in range(M_BLOCKS):
+            pooled = held.tile([P, POOLED], F32, name=f"pooled{m}")
+            for i in range(PIECES):
+                sums = sum_psum.tile([P, PIECE], F32)
+                picked = offsets[:, i * PIECE_OFFS : (i + 1) * PIECE_OFFS]
+                for k in range(K_BLOCKS):
+                    nc.tensor.matmul(
+                        sums[:],
+                        weights[:, k, m * P : (m + 1) * P],
+                        windows[k][:].indirect(picked),
+                        start=k == 0,
+                        stop=k == K_BLOCKS - 1,
+                    )
+                z = epilogue.tile([P, PIECE], F32)
+                nc.scalar.activation(z[:], sums[:], GELU, bias=bias[:, m : m + 1])
+                nc.vector.tensor_reduce(
+                    pooled[:, i * PIECE_POOLED : (i + 1) * PIECE_POOLED],
+                    z[:].rearrange("p (v t) -> p v t", t=NEIGHBOURS),
+                    mybir.AxisListType.X,
+                    mybir.AluOpType.max,
+                )
+            nc.sync.dma_start(out[m * P : (m + 1) * P, :], pooled[:])

@@ -13,6 +13,8 @@ PIECES = ENTRIES // PIECE
 PIECE_OFFS = PIECE // 16
 PIECE_POOLED = PIECE // NEIGHBOURS
 POOLED = ENTRIES // NEIGHBOURS
+BANK = 512
+WARM_UPS = 4
 
 FLOPS = 2 * FEATURES * OUTPUTS * ENTRIES
 
@@ -41,6 +43,12 @@ def tile_gather_matmul_kernel(tc, table, w, b, offs, out):
         nc.vector.memset(zero[:], 0.0)
         warm = held.tile([P, 1], F32)
         nc.scalar.activation(warm[:], zero[:], GELU, bias=zero[:])
+
+        blank = held.tile([P, BANK], BF16)
+        nc.vector.memset(blank[:], 0.0)
+        unread = flip_psum.tile([P, BANK], F32, tag=f"flipped{K_BLOCKS - 1}")
+        for turn in range(WARM_UPS):
+            nc.tensor.matmul(unread[:], blank[:, :P], blank[:], start=True, stop=True)
 
         windows = []
         for k in range(K_BLOCKS):

@@ -11,7 +11,6 @@ PIECE = 256
 NODE_BLOCKS, K_BLOCKS, M_BLOCKS = NODES // P, FEATURES // P, OUTPUTS // P
 PIECES = ENTRIES // PIECE
 PIECE_OFFS = PIECE // 16
-PIECE_POOLED = PIECE // NEIGHBOURS
 POOLED = ENTRIES // NEIGHBOURS
 BANK = 512
 WARM_UPS = 4
@@ -29,10 +28,10 @@ def tile_gather_matmul_kernel(tc, table, w, b, offs, out):
     ):
         rows = held.tile([P, NODE_BLOCKS, FEATURES], BF16)
         nc.sync.dma_start(rows[:], table.rearrange("(n p) k -> p n k", p=P))
+        weights = held.tile([P, K_BLOCKS, OUTPUTS], BF16)
+        nc.sync.dma_start(weights[:], w.rearrange("(k p) m -> p k m", p=P))
         offsets = held.tile([P, ENTRIES // 16], U16)
         nc.sync.dma_start(offsets[:], offs)
-        weights = held.tile([P, K_BLOCKS, OUTPUTS], BF16)
-        nc.scalar.dma_start(weights[:], w.rearrange("(k p) m -> p k m", p=P))
         bias = held.tile([P, M_BLOCKS], F32)
         nc.scalar.dma_start(bias[:], b.rearrange("(m p) o -> p (m o)", p=P))
 
@@ -75,12 +74,16 @@ def tile_gather_matmul_kernel(tc, table, w, b, offs, out):
                         start=k == 0,
                         stop=k == K_BLOCKS - 1,
                     )
-                z = epilogue.tile([P, PIECE], F32)
-                nc.scalar.activation(z[:], sums[:], GELU, bias=bias[:, m : m + 1])
-                nc.vector.tensor_reduce(
-                    pooled[:, i * PIECE_POOLED : (i + 1) * PIECE_POOLED],
-                    z[:].rearrange("p (v t) -> p v t", t=NEIGHBOURS),
-                    mybir.AxisListType.X,
-                    mybir.AluOpType.max,
-                )
+                last = m == M_BLOCKS - 1 and i == PIECES - 1
+                width = PIECE // 2 if last else PIECE
+                for start in range(0, PIECE, width):
+                    z = epilogue.tile([P, width], F32)
+                    nc.scalar.activation(z[:], sums[:, start : start + width], GELU, bias=bias[:, m : m + 1])
+                    first_node = (i * PIECE + start) // NEIGHBOURS
+                    nc.vector.tensor_reduce(
+                        pooled[:, first_node : first_node + width // NEIGHBOURS],
+                        z[:].rearrange("p (v t) -> p v t", t=NEIGHBOURS),
+                        mybir.AxisListType.X,
+                        mybir.AluOpType.max,
+                    )
             nc.sync.dma_start(out[m * P : (m + 1) * P, :], pooled[:])

@@ -33,18 +33,19 @@ def tile_gather_matmul_kernel(tc, table, w, b, offs, out):
         offsets = held.tile([P, ENTRIES // 16], U16)
         nc.sync.dma_start(offsets[:], offs)
         bias = held.tile([P, M_BLOCKS], F32)
-        nc.scalar.dma_start(bias[:], b.rearrange("(m p) o -> p (m o)", p=P))
+        nc.sync.dma_start(bias[:], b.rearrange("(m p) o -> p (m o)", p=P))
 
         identity = held.tile([P, P], BF16)
         make_identity(nc, identity[:])
+
+        blank = held.tile([P, BANK], BF16)
+        nc.vector.memset(blank[:], 0.0)
 
         zero = held.tile([P, 1], F32)
         nc.vector.memset(zero[:], 0.0)
         warm = held.tile([P, 1], F32)
         nc.scalar.activation(warm[:], zero[:], GELU, bias=zero[:])
 
-        blank = held.tile([P, BANK], BF16)
-        nc.vector.memset(blank[:], 0.0)
         unread = flip_psum.tile([P, BANK], F32, tag=f"flipped{K_BLOCKS - 1}")
         for turn in range(WARM_UPS):
             nc.tensor.matmul(unread[:], blank[:, :P], blank[:], start=True, stop=True)

@@ -13,7 +13,7 @@ PIECES = ENTRIES // PIECE
 PIECE_OFFS = PIECE // 16
 POOLED = ENTRIES // NEIGHBOURS
 BANK = 512
-WARM_UPS = 4
+WARM_UPS = 3
 
 FLOPS = 2 * FEATURES * OUTPUTS * ENTRIES
 

import concourse.mybir as mybir
from concourse.masks import make_identity

F32, BF16, U16 = mybir.dt.float32, mybir.dt.bfloat16, mybir.dt.uint16
GELU = mybir.ActivationFunctionType.Gelu_apprx_tanh

P = 128
NODES, FEATURES, OUTPUTS = 512, 256, 256
ENTRIES, NEIGHBOURS = 768, 8
PIECE = 256
NODE_BLOCKS, K_BLOCKS, M_BLOCKS = NODES // P, FEATURES // P, OUTPUTS // P
PIECES = ENTRIES // PIECE
PIECE_OFFS = PIECE // 16
POOLED = ENTRIES // NEIGHBOURS
BANK = 512
WARM_UPS = 3

FLOPS = 2 * FEATURES * OUTPUTS * ENTRIES


def tile_gather_matmul_kernel(tc, table, w, b, offs, out):
    nc = tc.nc
    with (
        tc.tile_pool(name="held", bufs=1) as held,
        tc.tile_pool(name="epilogue", bufs=PIECES * M_BLOCKS) as epilogue,
        tc.psum_pool(name="flip_psum", bufs=1) as flip_psum,
        tc.psum_pool(name="sum_psum", bufs=PIECES * M_BLOCKS) as sum_psum,
    ):
        rows = held.tile([P, NODE_BLOCKS, FEATURES], BF16)
        nc.sync.dma_start(rows[:], table.rearrange("(n p) k -> p n k", p=P))
        weights = held.tile([P, K_BLOCKS, OUTPUTS], BF16)
        nc.sync.dma_start(weights[:], w.rearrange("(k p) m -> p k m", p=P))
        offsets = held.tile([P, ENTRIES // 16], U16)
        nc.sync.dma_start(offsets[:], offs)
        bias = held.tile([P, M_BLOCKS], F32)
        nc.sync.dma_start(bias[:], b.rearrange("(m p) o -> p (m o)", p=P))

        identity = held.tile([P, P], BF16)
        make_identity(nc, identity[:])

        blank = held.tile([P, BANK], BF16)
        nc.vector.memset(blank[:], 0.0)

        zero = held.tile([P, 1], F32)
        nc.vector.memset(zero[:], 0.0)
        warm = held.tile([P, 1], F32)
        nc.scalar.activation(warm[:], zero[:], GELU, bias=zero[:])

        unread = flip_psum.tile([P, BANK], F32, tag=f"flipped{K_BLOCKS - 1}")
        for turn in range(WARM_UPS):
            nc.tensor.matmul(unread[:], blank[:, :P], blank[:], start=True, stop=True)

        windows = []
        for k in range(K_BLOCKS):
            flipped = flip_psum.tile([P, NODES], BF16, name=f"flipped{k}")
            for n in range(NODE_BLOCKS):
                nc.tensor.transpose(flipped[:, n * P : (n + 1) * P], rows[:, n, k * P : (k + 1) * P], identity[:])
            window = held.tile([P, NODES], BF16, name=f"window{k}")
            if k % 2 == 0:
                nc.vector.tensor_copy(window[:], flipped[:])
            else:
                nc.scalar.copy(window[:], flipped[:])
            windows.append(window)

        for m in range(M_BLOCKS):
            pooled = held.tile([P, POOLED], F32, name=f"pooled{m}")
            for i in range(PIECES):
                sums = sum_psum.tile([P, PIECE], F32)
                picked = offsets[:, i * PIECE_OFFS : (i + 1) * PIECE_OFFS]
                for k in range(K_BLOCKS):
                    nc.tensor.matmul(
                        sums[:],
                        weights[:, k, m * P : (m + 1) * P],
                        windows[k][:].indirect(picked),
                        start=k == 0,
                        stop=k == K_BLOCKS - 1,
                    )
                last = m == M_BLOCKS - 1 and i == PIECES - 1
                width = PIECE // 2 if last else PIECE
                for start in range(0, PIECE, width):
                    z = epilogue.tile([P, width], F32)
                    nc.scalar.activation(z[:], sums[:, start : start + width], GELU, bias=bias[:, m : m + 1])
                    first_node = (i * PIECE + start) // NEIGHBOURS
                    nc.vector.tensor_reduce(
                        pooled[:, first_node : first_node + width // NEIGHBOURS],
                        z[:].rearrange("p (v t) -> p v t", t=NEIGHBOURS),
                        mybir.AxisListType.X,
                        mybir.AluOpType.max,
                    )
            nc.sync.dma_start(out[m * P : (m + 1) * P, :], pooled[:])
